import numpy as np
import ml_dtypes


def mxq(x, axis, fmt="e4m3"):
    dtype, down = {"e4m3": (ml_dtypes.float8_e4m3fn, 7), "e5m2": (ml_dtypes.float8_e5m2, 14)}[fmt]
    v = np.moveaxis(np.asarray(x, np.float32).astype(ml_dtypes.bfloat16).astype(np.float64), axis, -1)
    blocks = v.reshape(v.shape[:-1] + (-1, 32))
    amax = np.abs(blocks).max(-1, keepdims=True)
    byte = np.maximum(np.where(amax > 0, np.frexp(amax)[1] - 1 + 127, 0) - down, 1)
    scale = np.exp2(byte - 127.0)
    codes = (blocks / scale).astype(np.float32).astype(dtype).astype(np.float64)
    return np.moveaxis((codes * scale).reshape(v.shape), -1, axis)


WIDE = False


def mx_kscale(k):
    if not WIDE:
        return np.ones(k)
    levels = np.array([10, -10, 5, -5, 0])
    if k % 512:
        return np.exp2(np.random.permutation(np.resize(levels, k // 32))).repeat(32)
    a = np.empty((k // 512, 16))
    for p in range(k // 512):
        a[p, :8] = np.random.permutation(np.resize(levels, 8))
        for g in range(8):
            far = levels[np.abs(levels - a[p, g]) >= 10]
            a[p, g + 8] = far[np.random.randint(len(far))]
    return np.exp2(a.ravel()).repeat(32)


def f64(x):
    return np.asarray(x).astype(np.float64)


def striped(idx):
    return np.tile(idx.reshape(-1, 16).T, (8, 1)).astype(np.uint16)


def unstriped(offs):
    return offs[:16].T.reshape(-1).astype(np.int64)


def pack_weight(w):
    k, n = w.shape
    w = f64(np.asarray(w, np.float32).astype(ml_dtypes.bfloat16)).reshape(k // 32, 32, n)
    amax = np.abs(w).max(1)
    byte = np.clip(np.where(amax > 0, np.frexp(amax)[1] - 1 + 127 - 7, 1), 1, 254)
    scaled = (w * np.exp2(127.0 - byte)[:, None, :]).reshape(k, n).astype(np.float32)
    words = np.ascontiguousarray(scaled.reshape(k // 512, 128, 4, n).transpose(0, 1, 3, 2)).astype(ml_dtypes.float8_e4m3fn).view(np.uint8)
    return words, np.ascontiguousarray(byte.astype(np.uint8).reshape(k // 512, 16, n))


def unpack_weight(words, scales):
    g, p, n, _ = words.shape
    vals = np.ascontiguousarray(words).view(ml_dtypes.float8_e4m3fn).astype(np.float64) * np.repeat(np.exp2(scales.astype(np.float64) - 127.0), 8, axis=1)[..., None]
    return vals.transpose(0, 1, 3, 2).reshape(g * 512, n)


E2M1 = np.array([0.0, 0.5, 1.0, 1.5, 2.0, 3.0, 4.0, 6.0, -0.0, -0.5, -1.0, -1.5, -2.0, -3.0, -4.0, -6.0])


def pack_fp4(w):
    k, n = w.shape
    w = f64(np.asarray(w, np.float32).astype(ml_dtypes.bfloat16)).reshape(k // 32, 32, n)
    amax = np.abs(w).max(1)
    mant, ex = np.frexp(amax / 6.0)
    byte = np.clip(np.where(amax > 0, np.where(mant > 0.5, ex, ex - 1) + 127, 1), 1, 254)
    scaled = (w * np.exp2(127.0 - byte)[:, None, :]).reshape(k, n).astype(np.float32)
    c = np.ascontiguousarray(scaled.reshape(k // 512, 128, 4, n).transpose(0, 1, 3, 2)).astype(ml_dtypes.float4_e2m1fn).view(np.uint8) & 0xF
    words = (c[..., 0::2] | (c[..., 1::2] << 4)).reshape(k // 512, 128, 2 * n)
    return np.ascontiguousarray(words), np.ascontiguousarray(byte.astype(np.uint8).reshape(k // 512, 16, n))


def unpack_fp4(words, scales):
    g, _, n = scales.shape
    words = np.ascontiguousarray(words).reshape(g, 128, n, 2)
    nib = np.empty((g, 128, n, 4), np.uint8)
    nib[..., 0::2] = words & 0xF
    nib[..., 1::2] = words >> 4
    vals = E2M1[nib] * np.repeat(np.exp2(scales.astype(np.float64) - 127.0), 8, axis=1)[..., None]
    return vals.transpose(0, 1, 3, 2).reshape(g * 512, n)


K, T, S, D, N, H, V, U = 1024, 2048, 1024, 4, 256, 512, 256, 512


def setup_inputs():
    n = np.random.standard_normal
    s = mx_kscale(K)[:, None]
    u = mx_kscale(H)
    packed_xT = pack_weight(n((K, T)) * s)
    packed_w1 = pack_fp4(n((K, H)) / np.sqrt(K) / s)
    packed_w2 = pack_fp4(n((K, H)) / np.sqrt(K) / s)
    packed_w3 = pack_fp4(n((H, N)) / np.sqrt(H) / u[:, None])
    return {
        "x_words": packed_xT[0],
        "x_scales": packed_xT[1],
        "w1_words": packed_w1[0],
        "w1_scales": packed_w1[1],
        "w2_words": packed_w2[0],
        "w2_scales": packed_w2[1],
        "px": (1.5 * n((H, U))).astype(np.float32),
        "unit": (np.random.uniform(0.6, 1.4, (H, 1)) * u[:, None]).astype(np.float32),
        "w3_words": packed_w3[0],
        "w3_scales": packed_w3[1],
        "offs": striped(np.random.permutation(T)[:S]),
        "nd": striped(np.random.permutation(np.concatenate([np.arange(V), np.random.randint(0, V, U - V)]))),
    }


def reference(x_words, x_scales, w1_words, w1_scales, w2_words, w2_scales, px, unit, w3_words, w3_scales, offs, nd):
    xq = unpack_weight(x_words, x_scales)[:, unstriped(offs)]
    ms = unpack_fp4(w1_words, w1_scales).T @ xq
    mass = np.log(np.exp(ms) + 1.0) + 0.2
    mtot = mass.reshape(len(mass), -1, D).sum(axis=2)
    mn = mtot[:, unstriped(nd)]
    cx = unpack_fp4(w2_words, w2_scales).T @ xq
    mx_ = mass * cx
    com = (mx_.reshape(len(mx_), -1, D).sum(axis=2)) / mtot
    cn = com[:, unstriped(nd)]
    sep = f64(px) - cn
    r2 = (sep) ** 2 + 0.6
    mono = (mn * sep) / r2
    mq = mass * ((cx - np.repeat(com, D, axis=1)) ** 2)
    quad = mq.reshape(len(mq), -1, D).sum(axis=2)
    qn = quad[:, unstriped(nd)]
    qua = (qn * sep) / ((r2) ** 2)
    hid = f64(unit) * (mono * np.tanh(qua) - (qua / r2))
    return unpack_fp4(w3_words, w3_scales).T @ mxq(hid, 0, "e4m3")

@@ -1,0 +1,308 @@
+import math
+from contextlib import ExitStack
+
+import concourse.mybir as mybir
+from concourse.masks import make_identity
+
+K, T, S, D, N, H, V, U = 1024, 2048, 1024, 4, 256, 512, 256, 512
+FLOPS = 2 * (2 * K * H * S + H * N * U)
+
+F32 = mybir.dt.float32
+BF16 = mybir.dt.bfloat16
+I32 = mybir.dt.int32
+U32 = mybir.dt.uint32
+U16 = mybir.dt.uint16
+U8 = mybir.dt.uint8
+FP8X4 = mybir.dt.float8_e4m3fn_x4
+FP4X4 = mybir.dt.float4_e2m1fn_x4
+ALU = mybir.AluOpType
+ACT = mybir.ActivationFunctionType
+
+P = 128
+PASSES = 2
+WIN = 528
+TINY = 1e-19
+
+
+def tile_picked_ynbodyt_mix_p_kernel(
+    tc, x_words, x_scales, w1_words, w1_scales, w2_words, w2_scales, px, unit, w3_words, w3_scales, offs, nd, out
+):
+    nc = tc.nc
+    with ExitStack() as ctx:
+        sb = ctx.enter_context(tc.tile_pool(name="sb", bufs=1))
+        ps = ctx.enter_context(tc.psum_pool(name="ps", bufs=1))
+
+        def sbuf(shape, dtype, name, tag=None):
+            return sb.tile(shape, dtype, name=name, tag=tag or name, align_bytes=64)
+
+        def bank(b, name):
+            return ps.tile([P, 512], F32, name=name, tag="bank%d" % b)
+
+        def load_scale_rows(queue, plane, scales):
+            for q in range(4):
+                queue.dma_start(
+                    out=plane[32 * q : 32 * q + 4].bitcast(I32),
+                    in_=scales[:, 4 * q : 4 * q + 4, :].rearrange("o r c -> r o c").bitcast(I32),
+                )
+
+        offs_sb = sbuf([P, S // 16], U16, "offs_sb")
+        nd_sb = sbuf([P, U // 16], U16, "nd_sb")
+        xs_win = sbuf([P, T], U8, "xs_win")
+        xs_pass1 = sbuf([P, S], U8, "xs_pass1")
+        nc.vector.memset(xs_win[:].bitcast(I32), 0)
+        nc.vector.memset(xs_pass1[:].bitcast(I32), 0)
+        nc.sync.dma_start(offs_sb[:], offs)
+        for q in range(4):
+            nc.scalar.dma_start(
+                out=xs_win[32 * q : 32 * q + 8].bitcast(I32), in_=x_scales[:, 4 * q : 4 * q + 4, :].bitcast(I32)
+            )
+        xw_win = [sbuf([P, T], I32, "xw_win%d" % o) for o in range(PASSES)]
+        nc.sync.dma_start(out=xw_win[0][:], in_=x_words[0].rearrange("p n t -> p (n t)").bitcast(I32))
+        nc.sync.dma_start(nd_sb[:], nd)
+        nc.sync.dma_start(out=xw_win[1][:], in_=x_words[1].rearrange("p n t -> p (n t)").bitcast(I32))
+
+        w1w = sbuf([P, PASSES, 2 * H], U8, "w1w")
+        w1s = sbuf([P, PASSES, H], U8, "w1s")
+        w2s = sbuf([P, PASSES, H], U8, "w2s")
+        w3s = sbuf([P, 1, N], U8, "w3s")
+        nc.gpsimd.dma_start(out=w1w[:].bitcast(I32), in_=w1_words.rearrange("o p c -> p o c").bitcast(I32))
+        nc.gpsimd.memset(w1s[:].bitcast(I32), 0)
+        load_scale_rows(nc.gpsimd, w1s, w1_scales)
+        ident = sbuf([P, P], F32, "ident")
+        make_identity(nc, ident[:])
+        mtot_w = [sbuf([P, WIN], F32, "mtot_w%d" % t) for t in range(4)]
+        ncom_w = [sbuf([P, WIN], F32, "ncom_w%d" % t) for t in range(4)]
+        quad_w = [sbuf([P, WIN], F32, "quad_w%d" % t) for t in range(4)]
+        for t in range(4):
+            for w in (ncom_w[t], mtot_w[t], quad_w[t]):
+                nc.gpsimd.memset(w[:, V:WIN], 0.0)
+            if t == 1:
+                nc.gpsimd.memset(w2s[:].bitcast(I32), 0)
+        nc.gpsimd.memset(w3s[:].bitcast(I32), 0)
+
+        xs_got = sbuf([P, S], U8, "xs_got")
+        xs_dealt = sbuf([P, S], U8, "xs_dealt")
+        nc.vector.tensor_copy(out=xs_got[:], in_=xs_win[:].indirect(offs_sb[:]))
+        nc.vector.tensor_copy(
+            out=xs_dealt[:].rearrange("p (g d v) -> p g d v", g=2, d=D),
+            in_=xs_got[:].rearrange("p (g v d) -> p g d v", g=2, d=D),
+        )
+        for lo, n in ((0, 64), (64, 32), (96, 4)):
+            nc.sync.dma_start(
+                out=xs_pass1[lo : lo + n].bitcast(I32), in_=xs_dealt[lo + 4 : lo + 4 + n].bitcast(I32)
+            )
+        load_scale_rows(nc.sync, w2s, w2_scales)
+        x_sc = [xs_dealt, xs_pass1]
+        xg = [sbuf([P, 2, D, P], U32, "xg%d" % o, tag=("xs_win", "xs_got")[o]) for o in range(PASSES)]
+        for g in range(2):
+            for o in range(PASSES):
+                nc.vector.tensor_copy(
+                    out=xg[o][:, g].rearrange("p d v -> p v d"),
+                    in_=xw_win[o][:].bitcast(U32).indirect(offs_sb[:, 32 * g : 32 * g + 32]),
+                )
+        w2w = sbuf([P, PASSES, 2 * H], U8, "w2w", tag="xw_win0")
+        nc.sync.dma_start(out=w2w[:].bitcast(I32), in_=w2_words.rearrange("o p c -> p o c").bitcast(I32))
+        px_sb = sbuf([P, 4, U], F32, "px_sb", tag="xw_win1")
+        nc.sync.dma_start(out=px_sb[:], in_=px.rearrange("(p t) r -> p t r", t=4))
+
+        def product(dst, g, d, words, scales, first, last):
+            c0 = 512 * g + P * d
+            for o in range(PASSES):
+                nc.tensor.matmul_mx(
+                    out=dst,
+                    lhsT=xg[o][:, g, d, :].bitcast(FP8X4),
+                    lhsT_scale=x_sc[o][:, c0 : c0 + P],
+                    rhs=words(o).bitcast(FP4X4),
+                    rhs_scale=scales(o),
+                    start=(o == 0),
+                    stop=(o == PASSES - 1),
+                )
+
+        sig = sbuf([P, 4, 8, P], F32, "sig")
+        xplus = [sbuf([P, 4, D, P], F32, "xplus%d" % g) for g in range(2)]
+        for g in range(2):
+            for d in range(D):
+                ms = bank(4 * g + d, "ms")
+                product(ms[:], g, d, lambda o: w1w[:, o, :], lambda o: w1s[:, o, :], True, True)
+                by_t = ms[:].rearrange("p (m t) -> p t m", t=4)
+                nc.scalar.activation(out=sig[:, :, 4 * g + d, :], in_=by_t, func=ACT.Sigmoid, scale=-1.0)
+                nc.vector.tensor_scalar(
+                    out=xplus[g][:, :, d, :], in0=by_t, scalar1=0.2, scalar2=None, op0=ALU.add
+                )
+
+        w2wd = sbuf([P, 2, PASSES, H], U8, "w2wd")
+        w2sd = sbuf([P, 2, PASSES, H // 2], U8, "w2sd")
+        nc.vector.tensor_copy(
+            out=w2wd[:].bitcast(I32).rearrange("p h o m -> p h (o m)"),
+            in_=w2w[:].bitcast(I32).rearrange("p o (m h) -> p h (o m)", h=2),
+        )
+        nc.vector.tensor_copy(
+            out=w2sd[:].rearrange("p h o (m e) -> p h (o m) e", e=2),
+            in_=w2s[:].rearrange("p o (m h e) -> p h (o m) e", h=2, e=2),
+        )
+        cx = {}
+        for h in range(2):
+            for g in range(2):
+                for pair in range(2):
+                    cx[h, g, pair] = bank(4 * h + 2 * g + pair, "cx")
+                    for a in range(2):
+                        product(
+                            cx[h, g, pair][:, 256 * a : 256 * a + 256], g, 2 * pair + a,
+                            lambda o: w2wd[:, h, o, :], lambda o: w2sd[:, h, o, :], True, True,
+                        )
+
+        w3w = sbuf([P, 2 * N], U8, "w3w", tag="xs_dealt")
+        unit_sb = sbuf([P, 4], F32, "unit_sb", tag="xs_pass1")
+        nc.sync.dma_start(out=unit_sb[:], in_=unit.rearrange("(p t) one -> p (t one)", t=4))
+        nc.sync.dma_start(out=w3w[:].bitcast(I32), in_=w3_words[0].bitcast(I32))
+        load_scale_rows(nc.sync, w3s, w3_scales)
+        for t in range(4):
+            lg = sig[:, t].rearrange("p k m -> p (k m)")
+            nc.scalar.activation(out=lg, in_=lg, func=ACT.Ln, scale=math.exp(-0.2), bias=TINY)
+
+        ebuf = sbuf([P, 4, U], F32, "ebuf", tag="xw_win0")
+        hbuf = sbuf([P, 4, U], F32, "hbuf")
+        sq = [sbuf([P, 2, U], F32, "sq%d" % h) for h in range(2)]
+        qua = [sbuf([P, 2, U], F32, "qua%d" % h) for h in range(2)]
+        mono = [sbuf([P, 2, U], F32, "mono%d" % h) for h in range(2)]
+        sep = [sbuf([P, U], F32, "sep%d" % t) for t in range(4)]
+        inv = [sbuf([P, U], F32, "inv%d" % t) for t in range(4)]
+        sir = [sbuf([P, U], F32, "sir%d" % t) for t in range(4)]
+
+        def children(h):
+            sums = [None, None, None]
+            for g in range(2):
+                mass = sbuf([P, 2, D, P], F32, "mass%d%d" % (h, g))
+                mc = sbuf([P, 2, D, P], F32, "mc%d%d" % (h, g))
+                mcc = sbuf([P, 2, D, P], F32, "mcc%d%d" % (h, g))
+                for e in range(2):
+                    t = 2 * h + e
+                    nc.vector.scalar_tensor_tensor(
+                        out=mass[:, e].rearrange("p d m -> p (d m)"),
+                        in0=sig[:, t, 4 * g : 4 * g + 4, :].rearrange("p d m -> p (d m)"),
+                        scalar=-1.0,
+                        in1=xplus[g][:, t].rearrange("p d m -> p (d m)"),
+                        op0=ALU.mult,
+                        op1=ALU.max,
+                    )
+                for src, dst in ((mass, mc), (mc, mcc)):
+                    for pair in range(2):
+                        nc.vector.tensor_tensor(
+                            out=dst[:, :, 2 * pair : 2 * pair + 2, :].rearrange("p e a m -> p a e m"),
+                            in0=src[:, :, 2 * pair : 2 * pair + 2, :].rearrange("p e a m -> p a e m"),
+                            in1=cx[h, g, pair][:].rearrange("p (a m e) -> p a e m", a=2, e=2),
+                            op=ALU.mult,
+                        )
+                for q, src in enumerate((mass, mc, mcc)):
+                    if g == 0:
+                        sums[q] = bank(4 * h + q, "sums")
+                    for e in range(2):
+                        c0 = V * e + P * g
+                        for d in range(D):
+                            nc.tensor.matmul(
+                                out=sums[q][:, c0 : c0 + P], lhsT=src[:, e, d, :], rhs=ident[:],
+                                start=(d == 0), stop=(d == D - 1), is_transpose=True,
+                            )
+            return sums
+
+        def nodes(h, sums):
+            rm = sbuf([P, 2 * V], F32, "rm%d" % h)
+            tmp = sbuf([P, 2 * V], F32, "tmp%d" % h)
+            nc.scalar.activation(out=rm[:], in_=sums[0][:], func=ACT.Square)
+            nc.scalar.activation(out=rm[:], in_=rm[:], func=ACT.Abs_reciprocal_sqrt)
+            nc.vector.tensor_tensor(out=tmp[:], in0=sums[0][:], in1=rm[:], op=ALU.mult)
+            nc.vector.scalar_tensor_tensor(
+                out=rm[:], in0=tmp[:], scalar=2.0, in1=rm[:], op0=ALU.subtract, op1=ALU.mult
+            )
+            for e in range(2):
+                t, cols = 2 * h + e, slice(V * e, V * e + V)
+                nc.vector.tensor_tensor(out=ncom_w[t][:, 0:V], in0=sums[1][:, cols], in1=rm[:, cols], op=ALU.mult)
+            for e in range(2):
+                t, cols = 2 * h + e, slice(V * e, V * e + V)
+                nc.scalar.activation(
+                    out=mtot_w[t][:, 0:V], in_=sums[0][:, cols], func=ACT.Copy, scale=unit_sb[:, t : t + 1]
+                )
+                nc.vector.tensor_tensor(out=tmp[:, cols], in0=sums[1][:, cols], in1=ncom_w[t][:, 0:V], op=ALU.mult)
+            for e in range(2):
+                t, cols = 2 * h + e, slice(V * e, V * e + V)
+                nc.vector.tensor_tensor(out=quad_w[t][:, 0:V], in0=sums[2][:, cols], in1=tmp[:, cols], op=ALU.add)
+
+        def separation(h):
+            for e in range(2):
+                t = 2 * h + e
+                if h == 0:
+                    nc.scalar.activation(out=sep[t][:], in_=ncom_w[t][:].indirect(nd_sb[:]), func=ACT.Copy)
+                    nc.vector.tensor_tensor(out=sep[t][:], in0=sep[t][:], in1=px_sb[:, t, :], op=ALU.add)
+                else:
+                    nc.vector.tensor_tensor(
+                        out=sep[t][:], in0=ncom_w[t][:].indirect(nd_sb[:]), in1=px_sb[:, t, :], op=ALU.add
+                    )
+            for e in range(2):
+                t = 2 * h + e
+                nc.scalar.activation(out=sq[h][:, e, :], in_=sep[t][:], func=ACT.Square)
+                nc.scalar.activation(out=sq[h][:, e, :], in_=sq[h][:, e, :], func=ACT.Square, bias=0.6)
+                nc.scalar.activation(out=inv[t][:], in_=sq[h][:, e, :], func=ACT.Abs_reciprocal_sqrt)
+            for e in range(2):
+                t = 2 * h + e
+                nc.scalar.activation(out=qua[h][:, e, :], in_=quad_w[t][:].indirect(nd_sb[:]), func=ACT.Copy)
+            for e in range(2):
+                t = 2 * h + e
+                nc.scalar.activation(out=mono[h][:, e, :], in_=mtot_w[t][:].indirect(nd_sb[:]), func=ACT.Copy)
+
+        def forces(h):
+            ts = (2 * h, 2 * h + 1)
+            for t in ts:
+                nc.vector.tensor_tensor(out=sir[t][:], in0=sep[t][:], in1=inv[t][:], op=ALU.mult)
+            for t in ts:
+                nc.vector.tensor_tensor(out=sep[t][:], in0=sir[t][:], in1=inv[t][:], op=ALU.mult)
+            for t in ts:
+                nc.vector.tensor_tensor(out=qua[h][:, t % 2, :], in0=qua[h][:, t % 2, :], in1=sep[t][:], op=ALU.mult)
+            for t in ts:
+                nc.vector.scalar_tensor_tensor(
+                    out=ebuf[:, t, :], in0=qua[h][:, t % 2, :], scalar=unit_sb[:, t : t + 1], in1=inv[t][:],
+                    op0=ALU.mult, op1=ALU.mult,
+                )
+            for t in ts:
+                nc.vector.tensor_tensor(out=mono[h][:, t % 2, :], in0=mono[h][:, t % 2, :], in1=sir[t][:], op=ALU.mult)
+
+        sums0 = children(0)
+        nodes(0, sums0)
+        separation(0)
+        sums1 = children(1)
+        nodes(1, sums1)
+        separation(1)
+        forces(0)
+        forces(1)
+
+        nc.scalar.activation(out=sq[1][:], in_=qua[0][:], func=ACT.Tanh)
+        nc.vector.tensor_tensor(out=hbuf[:, 0:2, :], in0=mono[0][:], in1=sq[1][:], op=ALU.mult)
+        for c in range(2):
+            cols = slice(256 * c, 256 * c + 256)
+            nc.scalar.activation(out=sq[0][:, :, cols], in_=qua[1][:, :, cols], func=ACT.Tanh)
+            nc.vector.tensor_tensor(out=hbuf[:, 2:4, cols], in0=mono[1][:, :, cols], in1=sq[0][:, :, cols], op=ALU.mult)
+        for c in range(2):
+            cols = slice(256 * c, 256 * c + 256)
+            hid = sbuf([P, 256, 4], BF16, "hid%d" % c)
+            codes = sbuf([P, 256], U32, "codes%d" % c)
+            hscale = sbuf([P, 256], U8, "hscale%d" % c)
+            nc.vector.tensor_tensor(
+                out=hid[:].rearrange("p (c i) t -> p c t i", i=4),
+                in0=hbuf[:, :, cols].rearrange("p t (c i) -> p c t i", i=4),
+                in1=ebuf[:, :, cols].rearrange("p t (c i) -> p c t i", i=4),
+                op=ALU.subtract,
+            )
+            nc.vector.quantize_mx(out=codes[:].bitcast(FP8X4), scales=hscale[:], in_=hid[:].rearrange("p r t -> p (r t)"))
+            acc = bank(3 + 4 * c, "acc")
+            for b in range(2):
+                nc.tensor.matmul_mx(
+                    out=acc[:, 256 * b : 256 * b + 256],
+                    lhsT=w3w[:, 256 * b : 256 * b + 256].bitcast(FP4X4),
+                    lhsT_scale=w3s[:, 0, P * b : P * b + P],
+                    rhs=codes[:].bitcast(FP8X4),
+                    rhs_scale=hscale[:],
+                    start=True,
+                    stop=True,
+                )
+            res = sbuf([P, 2, 256], F32, "res%d" % c)
+            nc.scalar.copy(out=res[:].rearrange("p b r -> p (b r)"), in_=acc[:])
+            nc.sync.dma_start(out=out.rearrange("(b m) r -> m b r", b=2)[:, :, cols], in_=res[:])

@@ -49,25 +49,28 @@ def tile_picked_ynbodyt_mix_p_kernel(
         nd_sb = sbuf([P, U // 16], U16, "nd_sb")
         xs_win = sbuf([P, T], U8, "xs_win")
         xs_pass1 = sbuf([P, S], U8, "xs_pass1")
-        nc.vector.memset(xs_win[:].bitcast(I32), 0)
-        nc.vector.memset(xs_pass1[:].bitcast(I32), 0)
+        w1w = sbuf([P, PASSES, 2 * H], U8, "w1w")
+        w1s = sbuf([P, PASSES, H], U8, "w1s")
+        w2w = sbuf([P, PASSES, 2 * H], U8, "w2w")
+        w2s = sbuf([P, PASSES, H], U8, "w2s")
+        w3w = sbuf([P, 2 * N], U8, "w3w")
+        w3s = sbuf([P, 1, N], U8, "w3s")
+        unit_sb = sbuf([P, 4], F32, "unit_sb")
+        nc.gpsimd.memset(xs_win[:].bitcast(I32), 0)
+        for plane in (w1s, xs_pass1, w2s, w3s):
+            nc.vector.memset(plane[:].bitcast(I32), 0)
         nc.sync.dma_start(offs_sb[:], offs)
+        nc.sync.dma_start(nd_sb[:], nd)
         for q in range(4):
-            nc.scalar.dma_start(
+            nc.sync.dma_start(
                 out=xs_win[32 * q : 32 * q + 8].bitcast(I32), in_=x_scales[:, 4 * q : 4 * q + 4, :].bitcast(I32)
             )
         xw_win = [sbuf([P, T], I32, "xw_win%d" % o) for o in range(PASSES)]
         nc.sync.dma_start(out=xw_win[0][:], in_=x_words[0].rearrange("p n t -> p (n t)").bitcast(I32))
-        nc.sync.dma_start(nd_sb[:], nd)
+        nc.sync.dma_start(out=w1w[:].bitcast(I32), in_=w1_words.rearrange("o p c -> p o c").bitcast(I32))
+        load_scale_rows(nc.sync, w1s, w1_scales)
         nc.sync.dma_start(out=xw_win[1][:], in_=x_words[1].rearrange("p n t -> p (n t)").bitcast(I32))
 
-        w1w = sbuf([P, PASSES, 2 * H], U8, "w1w")
-        w1s = sbuf([P, PASSES, H], U8, "w1s")
-        w2s = sbuf([P, PASSES, H], U8, "w2s")
-        w3s = sbuf([P, 1, N], U8, "w3s")
-        nc.gpsimd.dma_start(out=w1w[:].bitcast(I32), in_=w1_words.rearrange("o p c -> p o c").bitcast(I32))
-        nc.gpsimd.memset(w1s[:].bitcast(I32), 0)
-        load_scale_rows(nc.gpsimd, w1s, w1_scales)
         ident = sbuf([P, P], F32, "ident")
         make_identity(nc, ident[:])
         mtot_w = [sbuf([P, WIN], F32, "mtot_w%d" % t) for t in range(4)]
@@ -76,9 +79,6 @@ def tile_picked_ynbodyt_mix_p_kernel(
         for t in range(4):
             for w in (ncom_w[t], mtot_w[t], quad_w[t]):
                 nc.gpsimd.memset(w[:, V:WIN], 0.0)
-            if t == 1:
-                nc.gpsimd.memset(w2s[:].bitcast(I32), 0)
-        nc.gpsimd.memset(w3s[:].bitcast(I32), 0)
 
         xs_got = sbuf([P, S], U8, "xs_got")
         xs_dealt = sbuf([P, S], U8, "xs_dealt")
@@ -92,6 +92,7 @@ def tile_picked_ynbodyt_mix_p_kernel(
                 out=xs_pass1[lo : lo + n].bitcast(I32), in_=xs_dealt[lo + 4 : lo + 4 + n].bitcast(I32)
             )
         load_scale_rows(nc.sync, w2s, w2_scales)
+        nc.sync.dma_start(out=w2w[:].bitcast(I32), in_=w2_words.rearrange("o p c -> p o c").bitcast(I32))
         x_sc = [xs_dealt, xs_pass1]
         xg = [sbuf([P, 2, D, P], U32, "xg%d" % o, tag=("xs_win", "xs_got")[o]) for o in range(PASSES)]
         for g in range(2):
@@ -100,12 +101,10 @@ def tile_picked_ynbodyt_mix_p_kernel(
                     out=xg[o][:, g].rearrange("p d v -> p v d"),
                     in_=xw_win[o][:].bitcast(U32).indirect(offs_sb[:, 32 * g : 32 * g + 32]),
                 )
-        w2w = sbuf([P, PASSES, 2 * H], U8, "w2w", tag="xw_win0")
-        nc.sync.dma_start(out=w2w[:].bitcast(I32), in_=w2_words.rearrange("o p c -> p o c").bitcast(I32))
         px_sb = sbuf([P, 4, U], F32, "px_sb", tag="xw_win1")
         nc.sync.dma_start(out=px_sb[:], in_=px.rearrange("(p t) r -> p t r", t=4))
 
-        def product(dst, g, d, words, scales, first, last):
+        def product(dst, g, d, words, scales):
             c0 = 512 * g + P * d
             for o in range(PASSES):
                 nc.tensor.matmul_mx(
@@ -118,41 +117,35 @@ def tile_picked_ynbodyt_mix_p_kernel(
                     stop=(o == PASSES - 1),
                 )
 
+        w2wd = sbuf([P, 4, PASSES, 2 * P], U8, "w2wd")
+        w2sd = sbuf([P, 4, PASSES, P], U8, "w2sd")
+        nc.vector.tensor_copy(
+            out=w2wd[:].rearrange("p t o (m b) -> p t (o m) b", b=2),
+            in_=w2w[:].rearrange("p o (m t b) -> p t (o m) b", t=4, b=2),
+        )
+        nc.vector.tensor_copy(
+            out=w2sd[:].rearrange("p t o m -> p t (o m)"),
+            in_=w2s[:].rearrange("p o (m t) -> p t (o m)", t=4),
+        )
         sig = sbuf([P, 4, 8, P], F32, "sig")
         xplus = [sbuf([P, 4, D, P], F32, "xplus%d" % g) for g in range(2)]
         for g in range(2):
             for d in range(D):
                 ms = bank(4 * g + d, "ms")
-                product(ms[:], g, d, lambda o: w1w[:, o, :], lambda o: w1s[:, o, :], True, True)
+                product(ms[:], g, d, lambda o: w1w[:, o, :], lambda o: w1s[:, o, :])
                 by_t = ms[:].rearrange("p (m t) -> p t m", t=4)
                 nc.scalar.activation(out=sig[:, :, 4 * g + d, :], in_=by_t, func=ACT.Sigmoid, scale=-1.0)
                 nc.vector.tensor_scalar(
                     out=xplus[g][:, :, d, :], in0=by_t, scalar1=0.2, scalar2=None, op0=ALU.add
                 )
 
-        w2wd = sbuf([P, 2, PASSES, H], U8, "w2wd")
-        w2sd = sbuf([P, 2, PASSES, H // 2], U8, "w2sd")
-        nc.vector.tensor_copy(
-            out=w2wd[:].bitcast(I32).rearrange("p h o m -> p h (o m)"),
-            in_=w2w[:].bitcast(I32).rearrange("p o (m h) -> p h (o m)", h=2),
-        )
-        nc.vector.tensor_copy(
-            out=w2sd[:].rearrange("p h o (m e) -> p h (o m) e", e=2),
-            in_=w2s[:].rearrange("p o (m h e) -> p h (o m) e", h=2, e=2),
-        )
         cx = {}
-        for h in range(2):
+        for t in range(4):
             for g in range(2):
-                for pair in range(2):
-                    cx[h, g, pair] = bank(4 * h + 2 * g + pair, "cx")
-                    for a in range(2):
-                        product(
-                            cx[h, g, pair][:, 256 * a : 256 * a + 256], g, 2 * pair + a,
-                            lambda o: w2wd[:, h, o, :], lambda o: w2sd[:, h, o, :], True, True,
-                        )
+                cx[t, g] = bank(2 * t + g, "cx")
+                for d in range(D):
+                    product(cx[t, g][:, P * d : P * d + P], g, d, lambda o: w2wd[:, t, o, :], lambda o: w2sd[:, t, o, :])
 
-        w3w = sbuf([P, 2 * N], U8, "w3w", tag="xs_dealt")
-        unit_sb = sbuf([P, 4], F32, "unit_sb", tag="xs_pass1")
         nc.sync.dma_start(out=unit_sb[:], in_=unit.rearrange("(p t) one -> p (t one)", t=4))
         nc.sync.dma_start(out=w3w[:].bitcast(I32), in_=w3_words[0].bitcast(I32))
         load_scale_rows(nc.sync, w3s, w3_scales)
@@ -161,141 +154,127 @@ def tile_picked_ynbodyt_mix_p_kernel(
             nc.scalar.activation(out=lg, in_=lg, func=ACT.Ln, scale=math.exp(-0.2), bias=TINY)
 
         ebuf = sbuf([P, 4, U], F32, "ebuf", tag="xw_win0")
-        hbuf = sbuf([P, 4, U], F32, "hbuf")
-        sq = [sbuf([P, 2, U], F32, "sq%d" % h) for h in range(2)]
-        qua = [sbuf([P, 2, U], F32, "qua%d" % h) for h in range(2)]
-        mono = [sbuf([P, 2, U], F32, "mono%d" % h) for h in range(2)]
+        hbuf = sbuf([P, 4, U], BF16, "hbuf")
+        qua = [sbuf([P, U], F32, "qua%d" % t) for t in range(4)]
+        th = [sbuf([P, U], F32, "th0")] + qua[0:3]
+        mn = [sbuf([P, U], F32, "mn%d" % t) for t in range(4)]
+        sir = [sbuf([P, U], F32, "sir%d" % t) for t in range(4)]
         sep = [sbuf([P, U], F32, "sep%d" % t) for t in range(4)]
         inv = [sbuf([P, U], F32, "inv%d" % t) for t in range(4)]
-        sir = [sbuf([P, U], F32, "sir%d" % t) for t in range(4)]
+        sums = {}
 
-        def children(h):
-            sums = [None, None, None]
+        def add_up(dst, src):
+            for d in range(D):
+                nc.tensor.matmul(
+                    out=dst, lhsT=src[:, P * d : P * d + P], rhs=ident[:],
+                    start=(d == 0), stop=(d == D - 1), is_transpose=True,
+                )
+
+        def children(t):
+            mass = [sbuf([P, 512], F32, "mass%d%d" % (t, g)) for g in range(2)]
+            mc = [sbuf([P, 512], F32, "mc%d%d" % (t, g)) for g in range(2)]
+            mcc = [sbuf([P, 512], F32, "mcc%d%d" % (t, g)) for g in range(2)]
             for g in range(2):
-                mass = sbuf([P, 2, D, P], F32, "mass%d%d" % (h, g))
-                mc = sbuf([P, 2, D, P], F32, "mc%d%d" % (h, g))
-                mcc = sbuf([P, 2, D, P], F32, "mcc%d%d" % (h, g))
-                for e in range(2):
-                    t = 2 * h + e
-                    nc.vector.scalar_tensor_tensor(
-                        out=mass[:, e].rearrange("p d m -> p (d m)"),
-                        in0=sig[:, t, 4 * g : 4 * g + 4, :].rearrange("p d m -> p (d m)"),
-                        scalar=-1.0,
-                        in1=xplus[g][:, t].rearrange("p d m -> p (d m)"),
-                        op0=ALU.mult,
-                        op1=ALU.max,
-                    )
-                for src, dst in ((mass, mc), (mc, mcc)):
-                    for pair in range(2):
-                        nc.vector.tensor_tensor(
-                            out=dst[:, :, 2 * pair : 2 * pair + 2, :].rearrange("p e a m -> p a e m"),
-                            in0=src[:, :, 2 * pair : 2 * pair + 2, :].rearrange("p e a m -> p a e m"),
-                            in1=cx[h, g, pair][:].rearrange("p (a m e) -> p a e m", a=2, e=2),
-                            op=ALU.mult,
-                        )
-                for q, src in enumerate((mass, mc, mcc)):
-                    if g == 0:
-                        sums[q] = bank(4 * h + q, "sums")
-                    for e in range(2):
-                        c0 = V * e + P * g
-                        for d in range(D):
-                            nc.tensor.matmul(
-                                out=sums[q][:, c0 : c0 + P], lhsT=src[:, e, d, :], rhs=ident[:],
-                                start=(d == 0), stop=(d == D - 1), is_transpose=True,
-                            )
-            return sums
-
-        def nodes(h, sums):
-            rm = sbuf([P, 2 * V], F32, "rm%d" % h)
-            tmp = sbuf([P, 2 * V], F32, "tmp%d" % h)
-            nc.scalar.activation(out=rm[:], in_=sums[0][:], func=ACT.Square)
-            nc.scalar.activation(out=rm[:], in_=rm[:], func=ACT.Abs_reciprocal_sqrt)
-            nc.vector.tensor_tensor(out=tmp[:], in0=sums[0][:], in1=rm[:], op=ALU.mult)
-            nc.vector.scalar_tensor_tensor(
-                out=rm[:], in0=tmp[:], scalar=2.0, in1=rm[:], op0=ALU.subtract, op1=ALU.mult
-            )
-            for e in range(2):
-                t, cols = 2 * h + e, slice(V * e, V * e + V)
-                nc.vector.tensor_tensor(out=ncom_w[t][:, 0:V], in0=sums[1][:, cols], in1=rm[:, cols], op=ALU.mult)
-            for e in range(2):
-                t, cols = 2 * h + e, slice(V * e, V * e + V)
-                nc.scalar.activation(
-                    out=mtot_w[t][:, 0:V], in_=sums[0][:, cols], func=ACT.Copy, scale=unit_sb[:, t : t + 1]
-                )
-                nc.vector.tensor_tensor(out=tmp[:, cols], in0=sums[1][:, cols], in1=ncom_w[t][:, 0:V], op=ALU.mult)
-            for e in range(2):
-                t, cols = 2 * h + e, slice(V * e, V * e + V)
-                nc.vector.tensor_tensor(out=quad_w[t][:, 0:V], in0=sums[2][:, cols], in1=tmp[:, cols], op=ALU.add)
-
-        def separation(h):
-            for e in range(2):
-                t = 2 * h + e
-                if h == 0:
-                    nc.scalar.activation(out=sep[t][:], in_=ncom_w[t][:].indirect(nd_sb[:]), func=ACT.Copy)
-                    nc.vector.tensor_tensor(out=sep[t][:], in0=sep[t][:], in1=px_sb[:, t, :], op=ALU.add)
-                else:
-                    nc.vector.tensor_tensor(
-                        out=sep[t][:], in0=ncom_w[t][:].indirect(nd_sb[:]), in1=px_sb[:, t, :], op=ALU.add
-                    )
-            for e in range(2):
-                t = 2 * h + e
-                nc.scalar.activation(out=sq[h][:, e, :], in_=sep[t][:], func=ACT.Square)
-                nc.scalar.activation(out=sq[h][:, e, :], in_=sq[h][:, e, :], func=ACT.Square, bias=0.6)
-                nc.scalar.activation(out=inv[t][:], in_=sq[h][:, e, :], func=ACT.Abs_reciprocal_sqrt)
-            for e in range(2):
-                t = 2 * h + e
-                nc.scalar.activation(out=qua[h][:, e, :], in_=quad_w[t][:].indirect(nd_sb[:]), func=ACT.Copy)
-            for e in range(2):
-                t = 2 * h + e
-                nc.scalar.activation(out=mono[h][:, e, :], in_=mtot_w[t][:].indirect(nd_sb[:]), func=ACT.Copy)
-
-        def forces(h):
-            ts = (2 * h, 2 * h + 1)
-            for t in ts:
-                nc.vector.tensor_tensor(out=sir[t][:], in0=sep[t][:], in1=inv[t][:], op=ALU.mult)
-            for t in ts:
-                nc.vector.tensor_tensor(out=sep[t][:], in0=sir[t][:], in1=inv[t][:], op=ALU.mult)
-            for t in ts:
-                nc.vector.tensor_tensor(out=qua[h][:, t % 2, :], in0=qua[h][:, t % 2, :], in1=sep[t][:], op=ALU.mult)
-            for t in ts:
                 nc.vector.scalar_tensor_tensor(
-                    out=ebuf[:, t, :], in0=qua[h][:, t % 2, :], scalar=unit_sb[:, t : t + 1], in1=inv[t][:],
-                    op0=ALU.mult, op1=ALU.mult,
+                    out=mass[g][:],
+                    in0=sig[:, t, 4 * g : 4 * g + 4, :].rearrange("p d m -> p (d m)"),
+                    scalar=-1.0,
+                    in1=xplus[g][:, t].rearrange("p d m -> p (d m)"),
+                    op0=ALU.mult,
+                    op1=ALU.max,
                 )
-            for t in ts:
-                nc.vector.tensor_tensor(out=mono[h][:, t % 2, :], in0=mono[h][:, t % 2, :], in1=sir[t][:], op=ALU.mult)
+            for g in range(2):
+                nc.vector.tensor_tensor(out=mc[g][:], in0=mass[g][:], in1=cx[t, g][:], op=ALU.mult)
+            for g in range(2):
+                nc.vector.tensor_tensor(out=mcc[g][:], in0=mc[g][:], in1=cx[t, g][:], op=ALU.mult)
+            first, second = bank(2 * t, "sums_a"), bank(2 * t + 1, "sums_b")
+            for g in range(2):
+                add_up(first[:, P * g : P * g + P], mass[g])
+            for g in range(2):
+                add_up(second[:, P * g : P * g + P], mc[g])
+            for g in range(2):
+                add_up(second[:, V + P * g : V + P * g + P], mcc[g])
+            sums[t] = (first[:, 0:V], second[:, 0:V], second[:, V : 2 * V])
 
-        sums0 = children(0)
-        nodes(0, sums0)
-        separation(0)
-        sums1 = children(1)
-        nodes(1, sums1)
-        separation(1)
-        forces(0)
-        forces(1)
+        def nodes(t):
+            mtot, s1, s2 = sums[t]
+            rm = sbuf([P, V], F32, "rm%d" % t)
+            tmp = sbuf([P, V], F32, "tmp%d" % t)
+            nc.scalar.activation(out=rm[:], in_=mtot, func=ACT.Abs_reciprocal_sqrt)
+            nc.scalar.activation(out=mtot_w[t][:, 0:V], in_=mtot, func=ACT.Copy, scale=unit_sb[:, t : t + 1])
+            nc.scalar.activation(out=rm[:], in_=rm[:], func=ACT.Square)
+            nc.vector.tensor_tensor(out=tmp[:], in0=mtot, in1=rm[:], op=ALU.mult)
+            nc.vector.tensor_tensor(out=rm[:], in0=s1, in1=rm[:], op=ALU.mult)
+            nc.vector.scalar_tensor_tensor(
+                out=ncom_w[t][:, 0:V], in0=tmp[:], scalar=2.0, in1=rm[:], op0=ALU.subtract, op1=ALU.mult
+            )
+            nc.vector.tensor_tensor(out=tmp[:], in0=s1, in1=ncom_w[t][:, 0:V], op=ALU.mult)
+            nc.vector.tensor_tensor(out=quad_w[t][:, 0:V], in0=s2, in1=tmp[:], op=ALU.add)
 
-        nc.scalar.activation(out=sq[1][:], in_=qua[0][:], func=ACT.Tanh)
-        nc.vector.tensor_tensor(out=hbuf[:, 0:2, :], in0=mono[0][:], in1=sq[1][:], op=ALU.mult)
-        for c in range(2):
-            cols = slice(256 * c, 256 * c + 256)
-            nc.scalar.activation(out=sq[0][:, :, cols], in_=qua[1][:, :, cols], func=ACT.Tanh)
-            nc.vector.tensor_tensor(out=hbuf[:, 2:4, cols], in0=mono[1][:, :, cols], in1=sq[0][:, :, cols], op=ALU.mult)
-        for c in range(2):
-            cols = slice(256 * c, 256 * c + 256)
-            hid = sbuf([P, 256, 4], BF16, "hid%d" % c)
-            codes = sbuf([P, 256], U32, "codes%d" % c)
-            hscale = sbuf([P, 256], U8, "hscale%d" % c)
-            nc.vector.tensor_tensor(
+        def separation(t):
+            if t in ():
+                nc.vector.tensor_tensor(
+                    out=sep[t][:], in0=ncom_w[t][:].indirect(nd_sb[:]), in1=px_sb[:, t, :], op=ALU.add
+                )
+            else:
+                nc.scalar.activation(out=sep[t][:], in_=ncom_w[t][:].indirect(nd_sb[:]), func=ACT.Copy)
+                nc.vector.tensor_tensor(out=sep[t][:], in0=sep[t][:], in1=px_sb[:, t, :], op=ALU.add)
+            r4 = th[0] if t == 3 else inv[t]
+            nc.scalar.activation(out=r4[:], in_=sep[t][:], func=ACT.Square)
+            nc.scalar.activation(out=r4[:], in_=r4[:], func=ACT.Square, bias=0.6)
+            nc.scalar.activation(out=inv[t][:], in_=r4[:], func=ACT.Abs_reciprocal_sqrt)
+
+        def fetch_quad(t):
+            if t not in ():
+                nc.scalar.activation(out=qua[t][:], in_=quad_w[t][:].indirect(nd_sb[:]), func=ACT.Copy)
+
+        def fetch_mass(t):
+            if t not in ():
+                nc.scalar.activation(out=mn[t][:], in_=mtot_w[t][:].indirect(nd_sb[:]), func=ACT.Copy)
+
+        def forces(t):
+            nc.vector.tensor_tensor(out=sir[t][:], in0=sep[t][:], in1=inv[t][:], op=ALU.mult)
+            nc.vector.tensor_tensor(out=sep[t][:], in0=sir[t][:], in1=inv[t][:], op=ALU.mult)
+            qn = quad_w[t][:].indirect(nd_sb[:]) if t in () else qua[t][:]
+            nc.vector.tensor_tensor(out=qua[t][:], in0=qn, in1=sep[t][:], op=ALU.mult)
+
+        def terms(t):
+            nc.vector.scalar_tensor_tensor(
+                out=ebuf[:, t, :], in0=qua[t][:], scalar=unit_sb[:, t : t + 1], in1=inv[t][:],
+                op0=ALU.mult, op1=ALU.mult,
+            )
+            m = mtot_w[t][:].indirect(nd_sb[:]) if t in () else mn[t][:]
+            nc.vector.tensor_tensor(out=mn[t][:], in0=m, in1=sir[t][:], op=ALU.mult)
+
+        for t in range(4):
+            children(t)
+            nodes(t)
+            separation(t)
+            fetch_quad(t)
+        for t in range(4):
+            forces(t)
+        for t in range(4):
+            fetch_mass(t)
+            terms(t)
+        for t in range(4):
+            nc.scalar.activation(out=th[t][:], in_=qua[t][:], func=ACT.Tanh)
+            nc.vector.tensor_tensor(out=mn[t][:], in0=mn[t][:], in1=th[t][:], op=ALU.mult)
+            nc.vector.tensor_tensor(out=hbuf[:, t, :], in0=mn[t][:], in1=ebuf[:, t, :], op=ALU.subtract)
+        for c, (r0, n) in enumerate(((0, 128), (128, 128), (256, 128), (384, 128))):
+            cols = slice(r0, r0 + n)
+            hid = sbuf([P, n, 4], BF16, "hid%d" % c)
+            codes = sbuf([P, n], U32, "codes%d" % c)
+            hscale = sbuf([P, n], U8, "hscale%d" % c)
+            weave = nc.scalar.copy if ("V", "S", "V", "S")[c] == "S" else nc.vector.tensor_copy
+            weave(
                 out=hid[:].rearrange("p (c i) t -> p c t i", i=4),
-                in0=hbuf[:, :, cols].rearrange("p t (c i) -> p c t i", i=4),
-                in1=ebuf[:, :, cols].rearrange("p t (c i) -> p c t i", i=4),
-                op=ALU.subtract,
+                in_=hbuf[:, :, cols].rearrange("p t (c i) -> p c t i", i=4),
             )
             nc.vector.quantize_mx(out=codes[:].bitcast(FP8X4), scales=hscale[:], in_=hid[:].rearrange("p r t -> p (r t)"))
-            acc = bank(3 + 4 * c, "acc")
+            acc = bank(c, "acc")
             for b in range(2):
                 nc.tensor.matmul_mx(
-                    out=acc[:, 256 * b : 256 * b + 256],
+                    out=acc[:, n * b : n * b + n],
                     lhsT=w3w[:, 256 * b : 256 * b + 256].bitcast(FP4X4),
                     lhsT_scale=w3s[:, 0, P * b : P * b + P],
                     rhs=codes[:].bitcast(FP8X4),
@@ -303,6 +282,6 @@ def tile_picked_ynbodyt_mix_p_kernel(
                     start=True,
                     stop=True,
                 )
-            res = sbuf([P, 2, 256], F32, "res%d" % c)
-            nc.scalar.copy(out=res[:].rearrange("p b r -> p (b r)"), in_=acc[:])
+            res = sbuf([P, 2, n], F32, "res%d" % c)
+            nc.scalar.copy(out=res[:].rearrange("p b r -> p (b r)"), in_=acc[:, 0 : 2 * n])
             nc.sync.dma_start(out=out.rearrange("(b m) r -> m b r", b=2)[:, :, cols], in_=res[:])

@@ -56,7 +56,8 @@ def tile_picked_ynbodyt_mix_p_kernel(
         w3w = sbuf([P, 2 * N], U8, "w3w")
         w3s = sbuf([P, 1, N], U8, "w3s")
         unit_sb = sbuf([P, 4], F32, "unit_sb")
-        nc.gpsimd.memset(xs_win[:].bitcast(I32), 0)
+        nc.gpsimd.memset(xs_win[:, 0 : T // 2].bitcast(I32), 0)
+        nc.vector.memset(xs_win[:, T // 2 : T].bitcast(I32), 0)
         for plane in (w1s, xs_pass1, w2s, w3s):
             nc.vector.memset(plane[:].bitcast(I32), 0)
         nc.sync.dma_start(offs_sb[:], offs)
@@ -153,14 +154,14 @@ def tile_picked_ynbodyt_mix_p_kernel(
             lg = sig[:, t].rearrange("p k m -> p (k m)")
             nc.scalar.activation(out=lg, in_=lg, func=ACT.Ln, scale=math.exp(-0.2), bias=TINY)
 
-        ebuf = sbuf([P, 4, U], F32, "ebuf", tag="xw_win0")
-        hbuf = sbuf([P, 4, U], BF16, "hbuf")
-        qua = [sbuf([P, U], F32, "qua%d" % t) for t in range(4)]
-        th = [sbuf([P, U], F32, "th0")] + qua[0:3]
-        mn = [sbuf([P, U], F32, "mn%d" % t) for t in range(4)]
+        qua = sbuf([P, 4, U], F32, "qua", tag="xw_win0")
+        mono = sbuf([P, 4, U], F32, "mono", tag="xplus0")
+        ebuf = sbuf([P, 4, U], F32, "ebuf", tag="xplus1")
+        g2 = [sbuf([P, U], F32, "g2%d" % t) for t in range(4)]
         sir = [sbuf([P, U], F32, "sir%d" % t) for t in range(4)]
         sep = [sbuf([P, U], F32, "sep%d" % t) for t in range(4)]
         inv = [sbuf([P, U], F32, "inv%d" % t) for t in range(4)]
+        mn = {k: sbuf([P, U], F32, "mn%d" % k)[:] for k in range(1)}
         sums = {}
 
         def add_up(dst, src):
@@ -170,105 +171,145 @@ def tile_picked_ynbodyt_mix_p_kernel(
                     start=(d == 0), stop=(d == D - 1), is_transpose=True,
                 )
 
-        def children(t):
-            mass = [sbuf([P, 512], F32, "mass%d%d" % (t, g)) for g in range(2)]
-            mc = [sbuf([P, 512], F32, "mc%d%d" % (t, g)) for g in range(2)]
-            mcc = [sbuf([P, 512], F32, "mcc%d%d" % (t, g)) for g in range(2)]
-            for g in range(2):
-                nc.vector.scalar_tensor_tensor(
-                    out=mass[g][:],
-                    in0=sig[:, t, 4 * g : 4 * g + 4, :].rearrange("p d m -> p (d m)"),
-                    scalar=-1.0,
-                    in1=xplus[g][:, t].rearrange("p d m -> p (d m)"),
-                    op0=ALU.mult,
-                    op1=ALU.max,
-                )
-            for g in range(2):
-                nc.vector.tensor_tensor(out=mc[g][:], in0=mass[g][:], in1=cx[t, g][:], op=ALU.mult)
-            for g in range(2):
-                nc.vector.tensor_tensor(out=mcc[g][:], in0=mc[g][:], in1=cx[t, g][:], op=ALU.mult)
-            first, second = bank(2 * t, "sums_a"), bank(2 * t + 1, "sums_b")
-            for g in range(2):
-                add_up(first[:, P * g : P * g + P], mass[g])
-            for g in range(2):
-                add_up(second[:, P * g : P * g + P], mc[g])
-            for g in range(2):
-                add_up(second[:, V + P * g : V + P * g + P], mcc[g])
-            sums[t] = (first[:, 0:V], second[:, 0:V], second[:, V : 2 * V])
+        mass, mc, mcc = ([[sbuf([P, 512], F32, "%s%d%d" % (k, t, g)) for g in range(2)] for t in range(4)] for k in ("mass", "mc", "mcc"))
+        rm, chk, com0 = ([sbuf([P, V], F32, "%s%d" % (k, t)) for t in range(4)] for k in ("rm", "chk", "com0"))
+        r4 = inv[0:3] + [sbuf([P, U], F32, "r4_last")]
+        mult = lambda dst, x, y: nc.vector.tensor_tensor(out=dst, in0=x, in1=y, op=ALU.mult)
+        act = lambda dst, x, func, **kw: nc.scalar.activation(out=dst, in_=x, func=func, **kw)
 
-        def nodes(t):
-            mtot, s1, s2 = sums[t]
-            rm = sbuf([P, V], F32, "rm%d" % t)
-            tmp = sbuf([P, V], F32, "tmp%d" % t)
-            nc.scalar.activation(out=rm[:], in_=mtot, func=ACT.Abs_reciprocal_sqrt)
-            nc.scalar.activation(out=mtot_w[t][:, 0:V], in_=mtot, func=ACT.Copy, scale=unit_sb[:, t : t + 1])
-            nc.scalar.activation(out=rm[:], in_=rm[:], func=ACT.Square)
-            nc.vector.tensor_tensor(out=tmp[:], in0=mtot, in1=rm[:], op=ALU.mult)
-            nc.vector.tensor_tensor(out=rm[:], in0=s1, in1=rm[:], op=ALU.mult)
+        def v_mass(t, g):
             nc.vector.scalar_tensor_tensor(
-                out=ncom_w[t][:, 0:V], in0=tmp[:], scalar=2.0, in1=rm[:], op0=ALU.subtract, op1=ALU.mult
+                out=mass[t][g][:],
+                in0=sig[:, t, 4 * g : 4 * g + 4, :].rearrange("p d m -> p (d m)"),
+                scalar=-1.0,
+                in1=xplus[g][:, t].rearrange("p d m -> p (d m)"),
+                op0=ALU.mult,
+                op1=ALU.max,
             )
-            nc.vector.tensor_tensor(out=tmp[:], in0=s1, in1=ncom_w[t][:, 0:V], op=ALU.mult)
-            nc.vector.tensor_tensor(out=quad_w[t][:, 0:V], in0=s2, in1=tmp[:], op=ALU.add)
 
-        def separation(t):
-            if t in ():
-                nc.vector.tensor_tensor(
-                    out=sep[t][:], in0=ncom_w[t][:].indirect(nd_sb[:]), in1=px_sb[:, t, :], op=ALU.add
-                )
+        def v_mc(t, g):
+            mult(mc[t][g][:], mass[t][g][:], cx[t, g][:])
+
+        def v_mcc(t, g):
+            mult(mcc[t][g][:], mc[t][g][:], cx[t, g][:])
+            if g == 0:
+                first = bank(2 * t, "sums_a")
+                sums[t, 0] = first[:, 0:V]
+                for k in range(2):
+                    add_up(first[:, P * k : P * k + P], mass[t][k])
             else:
-                nc.scalar.activation(out=sep[t][:], in_=ncom_w[t][:].indirect(nd_sb[:]), func=ACT.Copy)
-                nc.vector.tensor_tensor(out=sep[t][:], in0=sep[t][:], in1=px_sb[:, t, :], op=ALU.add)
-            r4 = th[0] if t == 3 else inv[t]
-            nc.scalar.activation(out=r4[:], in_=sep[t][:], func=ACT.Square)
-            nc.scalar.activation(out=r4[:], in_=r4[:], func=ACT.Square, bias=0.6)
-            nc.scalar.activation(out=inv[t][:], in_=r4[:], func=ACT.Abs_reciprocal_sqrt)
+                second = bank(2 * t + 1, "sums_b")
+                sums[t, 1], sums[t, 2] = second[:, 0:V], second[:, V : 2 * V]
+                for q, src in enumerate((mc, mcc)):
+                    for k in range(2):
+                        add_up(second[:, V * q + P * k : V * q + P * k + P], src[t][k])
 
-        def fetch_quad(t):
-            if t not in ():
-                nc.scalar.activation(out=qua[t][:], in_=quad_w[t][:].indirect(nd_sb[:]), func=ACT.Copy)
+        def s_root(t):
+            act(rm[t][:], sums[t, 0], ACT.Abs_reciprocal_sqrt)
 
-        def fetch_mass(t):
-            if t not in ():
-                nc.scalar.activation(out=mn[t][:], in_=mtot_w[t][:].indirect(nd_sb[:]), func=ACT.Copy)
+        def s_recip(t):
+            act(rm[t][:], rm[t][:], ACT.Square)
+
+        def s_mtot(t):
+            act(mtot_w[t][:, 0:V], sums[t, 0], ACT.Copy, scale=unit_sb[:, t : t + 1])
+
+        def v_first(t):
+            mult(chk[t][:], sums[t, 0], rm[t][:])
+            mult(com0[t][:], sums[t, 1], rm[t][:])
+
+        def v_com(t):
+            nc.vector.scalar_tensor_tensor(
+                out=ncom_w[t][:, 0:V], in0=chk[t][:], scalar=2.0, in1=com0[t][:], op0=ALU.subtract, op1=ALU.mult
+            )
+
+        def v_cross(t):
+            mult(com0[t][:], sums[t, 1], ncom_w[t][:, 0:V])
+
+        def v_quad(t):
+            nc.vector.tensor_tensor(out=quad_w[t][:, 0:V], in0=sums[t, 2], in1=com0[t][:], op=ALU.add)
+
+        def s_com(t):
+            act(sep[t][:], ncom_w[t][:].indirect(nd_sb[:]), ACT.Copy)
+
+        def s_quad(t):
+            act(g2[t][:], quad_w[t][:].indirect(nd_sb[:]), ACT.Copy)
+
+        def s_mass(t):
+            if t == 1:
+                late = sbuf([P, 3, U], F32, "mn_late", tag="r4_last")
+                mn.update({k: late[:, k - 1, :] for k in range(1, 4)})
+            act(mn[t], mtot_w[t][:].indirect(nd_sb[:]), ACT.Copy)
+
+        def v_sep(t):
+            nc.vector.tensor_tensor(out=sep[t][:], in0=sep[t][:], in1=px_sb[:, t, :], op=ALU.add)
+
+        def s_sq(t):
+            act(r4[t][:], sep[t][:], ACT.Square)
+
+        def s_r4(t):
+            act(r4[t][:], r4[t][:], ACT.Square, bias=0.6)
+
+        def s_inv(t):
+            act(inv[t][:], r4[t][:], ACT.Abs_reciprocal_sqrt)
 
         def forces(t):
-            nc.vector.tensor_tensor(out=sir[t][:], in0=sep[t][:], in1=inv[t][:], op=ALU.mult)
-            nc.vector.tensor_tensor(out=sep[t][:], in0=sir[t][:], in1=inv[t][:], op=ALU.mult)
-            qn = quad_w[t][:].indirect(nd_sb[:]) if t in () else qua[t][:]
-            nc.vector.tensor_tensor(out=qua[t][:], in0=qn, in1=sep[t][:], op=ALU.mult)
+            mult(sir[t][:], sep[t][:], inv[t][:])
+            mult(sep[t][:], sir[t][:], inv[t][:])
+            mult(qua[:, t, :], g2[t][:], sep[t][:])
 
-        def terms(t):
+        def v_soft(t):
             nc.vector.scalar_tensor_tensor(
-                out=ebuf[:, t, :], in0=qua[t][:], scalar=unit_sb[:, t : t + 1], in1=inv[t][:],
-                op0=ALU.mult, op1=ALU.mult,
+                out=ebuf[:, t, :], in0=qua[:, t, :], scalar=unit_sb[:, t : t + 1], in1=inv[t][:], op0=ALU.mult, op1=ALU.mult
             )
-            m = mtot_w[t][:].indirect(nd_sb[:]) if t in () else mn[t][:]
-            nc.vector.tensor_tensor(out=mn[t][:], in0=m, in1=sir[t][:], op=ALU.mult)
 
-        for t in range(4):
-            children(t)
-            nodes(t)
-            separation(t)
-            fetch_quad(t)
+        def v_mono(t):
+            mult(mono[:, t, :], mn[t], sir[t][:])
+
+        def do(step, t, *more):
+            if 0 <= t < 4:
+                step(t, *more)
+
+        v_mass(0, 0)
+        for t in range(6):
+            do(v_mass, t, 1)
+            do(s_root, t - 1)
+            do(s_recip, t - 1)
+            do(s_mtot, t - 1)
+            do(v_mc, t, 0)
+            do(v_sep, t - 2)
+            do(s_sq, t - 2)
+            do(s_r4, t - 2)
+            do(s_inv, t - 2)
+            do(v_mc, t, 1)
+            do(v_first, t - 1)
+            do(v_mcc, t, 0)
+            do(v_com, t - 1)
+            do(s_com, t - 1)
+            do(v_mcc, t, 1)
+            do(v_cross, t - 1)
+            do(v_mass, t + 1, 0)
+            do(v_quad, t - 1)
+            do(s_quad, t - 1)
         for t in range(4):
             forces(t)
         for t in range(4):
-            fetch_mass(t)
-            terms(t)
+            s_mass(t)
+            v_soft(t)
         for t in range(4):
-            nc.scalar.activation(out=th[t][:], in_=qua[t][:], func=ACT.Tanh)
-            nc.vector.tensor_tensor(out=mn[t][:], in0=mn[t][:], in1=th[t][:], op=ALU.mult)
-            nc.vector.tensor_tensor(out=hbuf[:, t, :], in0=mn[t][:], in1=ebuf[:, t, :], op=ALU.subtract)
+            v_mono(t)
         for c, (r0, n) in enumerate(((0, 128), (128, 128), (256, 128), (384, 128))):
             cols = slice(r0, r0 + n)
             hid = sbuf([P, n, 4], BF16, "hid%d" % c)
             codes = sbuf([P, n], U32, "codes%d" % c)
             hscale = sbuf([P, n], U8, "hscale%d" % c)
-            weave = nc.scalar.copy if ("V", "S", "V", "S")[c] == "S" else nc.vector.tensor_copy
-            weave(
+            th = sbuf([P, 4, n], F32, "th%d" % c)
+            act(th[:], qua[:, :, cols], ACT.Tanh)
+            mult(th[:], th[:], mono[:, :, cols])
+            nc.vector.tensor_tensor(
                 out=hid[:].rearrange("p (c i) t -> p c t i", i=4),
-                in_=hbuf[:, :, cols].rearrange("p t (c i) -> p c t i", i=4),
+                in0=th[:].rearrange("p t (c i) -> p c t i", i=4),
+                in1=ebuf[:, :, cols].rearrange("p t (c i) -> p c t i", i=4),
+                op=ALU.subtract,
             )
             nc.vector.quantize_mx(out=codes[:].bitcast(FP8X4), scales=hscale[:], in_=hid[:].rearrange("p r t -> p (r t)"))
             acc = bank(c, "acc")

@@ -107,15 +107,15 @@ def tile_picked_ynbodyt_mix_p_kernel(
 
         def product(dst, g, d, words, scales):
             c0 = 512 * g + P * d
-            for o in range(PASSES):
+            for n, o in enumerate((g, 1 - g)):
                 nc.tensor.matmul_mx(
                     out=dst,
                     lhsT=xg[o][:, g, d, :].bitcast(FP8X4),
                     lhsT_scale=x_sc[o][:, c0 : c0 + P],
                     rhs=words(o).bitcast(FP4X4),
                     rhs_scale=scales(o),
-                    start=(o == 0),
-                    stop=(o == PASSES - 1),
+                    start=(n == 0),
+                    stop=(n == PASSES - 1),
                 )
 
         w2wd = sbuf([P, 4, PASSES, 2 * P], U8, "w2wd")
@@ -129,7 +129,7 @@ def tile_picked_ynbodyt_mix_p_kernel(
             in_=w2s[:].rearrange("p o (m t) -> p t (o m)", t=4),
         )
         sig = sbuf([P, 4, 8, P], F32, "sig")
-        xplus = [sbuf([P, 4, D, P], F32, "xplus%d" % g) for g in range(2)]
+        xplus = sbuf([P, 4, 8, P], F32, "xplus")
         for g in range(2):
             for d in range(D):
                 ms = bank(4 * g + d, "ms")
@@ -137,7 +137,7 @@ def tile_picked_ynbodyt_mix_p_kernel(
                 by_t = ms[:].rearrange("p (m t) -> p t m", t=4)
                 nc.scalar.activation(out=sig[:, :, 4 * g + d, :], in_=by_t, func=ACT.Sigmoid, scale=-1.0)
                 nc.vector.tensor_scalar(
-                    out=xplus[g][:, :, d, :], in0=by_t, scalar1=0.2, scalar2=None, op0=ALU.add
+                    out=xplus[:, :, 4 * g + d, :], in0=by_t, scalar1=0.2, scalar2=None, op0=ALU.add
                 )
 
         cx = {}
@@ -151,12 +151,13 @@ def tile_picked_ynbodyt_mix_p_kernel(
         nc.sync.dma_start(out=w3w[:].bitcast(I32), in_=w3_words[0].bitcast(I32))
         load_scale_rows(nc.sync, w3s, w3_scales)
         for t in range(4):
-            lg = sig[:, t].rearrange("p k m -> p (k m)")
-            nc.scalar.activation(out=lg, in_=lg, func=ACT.Ln, scale=math.exp(-0.2), bias=TINY)
+            for half in range(2):
+                lg = sig[:, t, :, 64 * half : 64 * half + 64]
+                nc.scalar.activation(out=lg, in_=lg, func=ACT.Ln, scale=math.exp(-0.2), bias=TINY)
 
         qua = sbuf([P, 4, U], F32, "qua", tag="xw_win0")
-        mono = sbuf([P, 4, U], F32, "mono", tag="xplus0")
-        ebuf = sbuf([P, 4, U], F32, "ebuf", tag="xplus1")
+        mono = sbuf([P, 4, U], F32, "mono", tag="xplus")
+        ebuf = sbuf([P, 4, U], F32, "ebuf", tag="sig")
         g2 = [sbuf([P, U], F32, "g2%d" % t) for t in range(4)]
         sir = [sbuf([P, U], F32, "sir%d" % t) for t in range(4)]
         sep = [sbuf([P, U], F32, "sep%d" % t) for t in range(4)]
@@ -171,7 +172,9 @@ def tile_picked_ynbodyt_mix_p_kernel(
                     start=(d == 0), stop=(d == D - 1), is_transpose=True,
                 )
 
-        mass, mc, mcc = ([[sbuf([P, 512], F32, "%s%d%d" % (k, t, g)) for g in range(2)] for t in range(4)] for k in ("mass", "mc", "mcc"))
+        mc, mcc = ([[sbuf([P, 512], F32, "%s%d%d" % (k, t, g))[:] for g in range(2)] for t in range(4)] for k in ("mc", "mcc"))
+        mass_t = [sbuf([P, 8, P], F32, "mass%d" % t) for t in range(4)]
+        mass = [[mass_t[t][:, 4 * g : 4 * g + 4, :].rearrange("p d m -> p (d m)") for g in range(2)] for t in range(4)]
         rm, chk, com0 = ([sbuf([P, V], F32, "%s%d" % (k, t)) for t in range(4)] for k in ("rm", "chk", "com0"))
         r4 = inv[0:3] + [sbuf([P, U], F32, "r4_last")]
         mult = lambda dst, x, y: nc.vector.tensor_tensor(out=dst, in0=x, in1=y, op=ALU.mult)
@@ -179,10 +182,10 @@ def tile_picked_ynbodyt_mix_p_kernel(
 
         def v_mass(t, g):
             nc.vector.scalar_tensor_tensor(
-                out=mass[t][g][:],
-                in0=sig[:, t, 4 * g : 4 * g + 4, :].rearrange("p d m -> p (d m)"),
+                out=mass_t[t][:, :, 64 * g : 64 * g + 64],
+                in0=sig[:, t, :, 64 * g : 64 * g + 64],
                 scalar=-1.0,
-                in1=xplus[g][:, t].rearrange("p d m -> p (d m)"),
+                in1=xplus[:, t, :, 64 * g : 64 * g + 64],
                 op0=ALU.mult,
                 op1=ALU.max,
             )
@@ -276,6 +279,7 @@ def tile_picked_ynbodyt_mix_p_kernel(
             do(s_recip, t - 1)
             do(s_mtot, t - 1)
             do(v_mc, t, 0)
+            do(forces, t - 4)
             do(v_sep, t - 2)
             do(s_sq, t - 2)
             do(s_r4, t - 2)
@@ -290,7 +294,7 @@ def tile_picked_ynbodyt_mix_p_kernel(
             do(v_mass, t + 1, 0)
             do(v_quad, t - 1)
             do(s_quad, t - 1)
-        for t in range(4):
+        for t in range(2, 4):
             forces(t)
         for t in range(4):
             s_mass(t)

import math
from contextlib import ExitStack

import concourse.mybir as mybir
from concourse.masks import make_identity

K, T, S, D, N, H, V, U = 1024, 2048, 1024, 4, 256, 512, 256, 512
FLOPS = 2 * (2 * K * H * S + H * N * U)

F32 = mybir.dt.float32
BF16 = mybir.dt.bfloat16
I32 = mybir.dt.int32
U32 = mybir.dt.uint32
U16 = mybir.dt.uint16
U8 = mybir.dt.uint8
FP8X4 = mybir.dt.float8_e4m3fn_x4
FP4X4 = mybir.dt.float4_e2m1fn_x4
ALU = mybir.AluOpType
ACT = mybir.ActivationFunctionType

P = 128
PASSES = 2
WIN = 528
TINY = 1e-19


def tile_picked_ynbodyt_mix_p_kernel(
    tc, x_words, x_scales, w1_words, w1_scales, w2_words, w2_scales, px, unit, w3_words, w3_scales, offs, nd, out
):
    nc = tc.nc
    with ExitStack() as ctx:
        sb = ctx.enter_context(tc.tile_pool(name="sb", bufs=1))
        ps = ctx.enter_context(tc.psum_pool(name="ps", bufs=1))

        def sbuf(shape, dtype, name, tag=None):
            return sb.tile(shape, dtype, name=name, tag=tag or name, align_bytes=64)

        def bank(b, name):
            return ps.tile([P, 512], F32, name=name, tag="bank%d" % b)

        def load_scale_rows(queue, plane, scales):
            for q in range(4):
                queue.dma_start(
                    out=plane[32 * q : 32 * q + 4].bitcast(I32),
                    in_=scales[:, 4 * q : 4 * q + 4, :].rearrange("o r c -> r o c").bitcast(I32),
                )

        offs_sb = sbuf([P, S // 16], U16, "offs_sb")
        nd_sb = sbuf([P, U // 16], U16, "nd_sb")
        xs_win = sbuf([P, T], U8, "xs_win")
        xs_pass1 = sbuf([P, S], U8, "xs_pass1")
        w1w = sbuf([P, PASSES, 2 * H], U8, "w1w")
        w1s = sbuf([P, PASSES, H], U8, "w1s")
        w2w = sbuf([P, PASSES, 2 * H], U8, "w2w")
        w2s = sbuf([P, PASSES, H], U8, "w2s")
        w3w = sbuf([P, 2 * N], U8, "w3w")
        w3s = sbuf([P, 1, N], U8, "w3s")
        unit_sb = sbuf([P, 4], F32, "unit_sb")
        nc.gpsimd.memset(xs_win[:, 0 : T // 2].bitcast(I32), 0)
        nc.vector.memset(xs_win[:, T // 2 : T].bitcast(I32), 0)
        for plane in (w1s, xs_pass1, w2s, w3s):
            nc.vector.memset(plane[:].bitcast(I32), 0)
        nc.sync.dma_start(offs_sb[:], offs)
        nc.sync.dma_start(nd_sb[:], nd)
        for q in range(4):
            nc.sync.dma_start(
                out=xs_win[32 * q : 32 * q + 8].bitcast(I32), in_=x_scales[:, 4 * q : 4 * q + 4, :].bitcast(I32)
            )
        xw_win = [sbuf([P, T], I32, "xw_win%d" % o) for o in range(PASSES)]
        nc.sync.dma_start(out=xw_win[0][:], in_=x_words[0].rearrange("p n t -> p (n t)").bitcast(I32))
        nc.sync.dma_start(out=w1w[:].bitcast(I32), in_=w1_words.rearrange("o p c -> p o c").bitcast(I32))
        load_scale_rows(nc.sync, w1s, w1_scales)
        nc.sync.dma_start(out=xw_win[1][:], in_=x_words[1].rearrange("p n t -> p (n t)").bitcast(I32))

        ident = sbuf([P, P], F32, "ident")
        make_identity(nc, ident[:])
        mtot_w = [sbuf([P, WIN], F32, "mtot_w%d" % t) for t in range(4)]
        ncom_w = [sbuf([P, WIN], F32, "ncom_w%d" % t) for t in range(4)]
        quad_w = [sbuf([P, WIN], F32, "quad_w%d" % t) for t in range(4)]
        for t in range(4):
            for w in (ncom_w[t], mtot_w[t], quad_w[t]):
                nc.gpsimd.memset(w[:, V:WIN], 0.0)

        xs_got = sbuf([P, S], U8, "xs_got")
        xs_dealt = sbuf([P, S], U8, "xs_dealt")
        nc.vector.tensor_copy(out=xs_got[:], in_=xs_win[:].indirect(offs_sb[:]))
        nc.vector.tensor_copy(
            out=xs_dealt[:].rearrange("p (g d v) -> p g d v", g=2, d=D),
            in_=xs_got[:].rearrange("p (g v d) -> p g d v", g=2, d=D),
        )
        for lo, n in ((0, 64), (64, 32), (96, 4)):
            nc.sync.dma_start(
                out=xs_pass1[lo : lo + n].bitcast(I32), in_=xs_dealt[lo + 4 : lo + 4 + n].bitcast(I32)
            )
        load_scale_rows(nc.sync, w2s, w2_scales)
        nc.sync.dma_start(out=w2w[:].bitcast(I32), in_=w2_words.rearrange("o p c -> p o c").bitcast(I32))
        x_sc = [xs_dealt, xs_pass1]
        xg = [sbuf([P, 2, D, P], U32, "xg%d" % o, tag=("xs_win", "xs_got")[o]) for o in range(PASSES)]
        for g in range(2):
            for o in range(PASSES):
                nc.vector.tensor_copy(
                    out=xg[o][:, g].rearrange("p d v -> p v d"),
                    in_=xw_win[o][:].bitcast(U32).indirect(offs_sb[:, 32 * g : 32 * g + 32]),
                )
        px_sb = sbuf([P, 4, U], F32, "px_sb", tag="xw_win1")
        nc.sync.dma_start(out=px_sb[:], in_=px.rearrange("(p t) r -> p t r", t=4))

        def product(dst, g, d, words, scales):
            c0 = 512 * g + P * d
            for n, o in enumerate((g, 1 - g)):
                nc.tensor.matmul_mx(
                    out=dst,
                    lhsT=xg[o][:, g, d, :].bitcast(FP8X4),
                    lhsT_scale=x_sc[o][:, c0 : c0 + P],
                    rhs=words(o).bitcast(FP4X4),
                    rhs_scale=scales(o),
                    start=(n == 0),
                    stop=(n == PASSES - 1),
                )

        w2wd = sbuf([P, 4, PASSES, 2 * P], U8, "w2wd")
        w2sd = sbuf([P, 4, PASSES, P], U8, "w2sd")
        nc.vector.tensor_copy(
            out=w2wd[:].rearrange("p t o (m b) -> p t (o m) b", b=2),
            in_=w2w[:].rearrange("p o (m t b) -> p t (o m) b", t=4, b=2),
        )
        nc.vector.tensor_copy(
            out=w2sd[:].rearrange("p t o m -> p t (o m)"),
            in_=w2s[:].rearrange("p o (m t) -> p t (o m)", t=4),
        )
        sig = sbuf([P, 4, 8, P], F32, "sig")
        xplus = sbuf([P, 4, 8, P], F32, "xplus")
        for g in range(2):
            for d in range(D):
                ms = bank(4 * g + d, "ms")
                product(ms[:], g, d, lambda o: w1w[:, o, :], lambda o: w1s[:, o, :])
                by_t = ms[:].rearrange("p (m t) -> p t m", t=4)
                nc.scalar.activation(out=sig[:, :, 4 * g + d, :], in_=by_t, func=ACT.Sigmoid, scale=-1.0)
                nc.vector.tensor_scalar(
                    out=xplus[:, :, 4 * g + d, :], in0=by_t, scalar1=0.2, scalar2=None, op0=ALU.add
                )

        cx = {}
        for t in range(4):
            for g in range(2):
                cx[t, g] = bank(2 * t + g, "cx")
                for d in range(D):
                    product(cx[t, g][:, P * d : P * d + P], g, d, lambda o: w2wd[:, t, o, :], lambda o: w2sd[:, t, o, :])

        nc.sync.dma_start(out=unit_sb[:], in_=unit.rearrange("(p t) one -> p (t one)", t=4))
        nc.sync.dma_start(out=w3w[:].bitcast(I32), in_=w3_words[0].bitcast(I32))
        load_scale_rows(nc.sync, w3s, w3_scales)
        for t in range(4):
            for half in range(2):
                lg = sig[:, t, :, 64 * half : 64 * half + 64]
                nc.scalar.activation(out=lg, in_=lg, func=ACT.Ln, scale=math.exp(-0.2), bias=TINY)

        qua = sbuf([P, 4, U], F32, "qua", tag="xw_win0")
        mono = sbuf([P, 4, U], F32, "mono", tag="xplus")
        ebuf = sbuf([P, 4, U], F32, "ebuf", tag="sig")
        g2 = [sbuf([P, U], F32, "g2%d" % t) for t in range(4)]
        sir = [sbuf([P, U], F32, "sir%d" % t) for t in range(4)]
        sep = [sbuf([P, U], F32, "sep%d" % t) for t in range(4)]
        inv = [sbuf([P, U], F32, "inv%d" % t) for t in range(4)]
        mn = {k: sbuf([P, U], F32, "mn%d" % k)[:] for k in range(1)}
        sums = {}

        def add_up(dst, src):
            for d in range(D):
                nc.tensor.matmul(
                    out=dst, lhsT=src[:, P * d : P * d + P], rhs=ident[:],
                    start=(d == 0), stop=(d == D - 1), is_transpose=True,
                )

        mc, mcc = ([[sbuf([P, 512], F32, "%s%d%d" % (k, t, g))[:] for g in range(2)] for t in range(4)] for k in ("mc", "mcc"))
        mass_t = [sbuf([P, 8, P], F32, "mass%d" % t) for t in range(4)]
        mass = [[mass_t[t][:, 4 * g : 4 * g + 4, :].rearrange("p d m -> p (d m)") for g in range(2)] for t in range(4)]
        rm, chk, com0 = ([sbuf([P, V], F32, "%s%d" % (k, t)) for t in range(4)] for k in ("rm", "chk", "com0"))
        r4 = inv[0:3] + [sbuf([P, U], F32, "r4_last")]
        mult = lambda dst, x, y: nc.vector.tensor_tensor(out=dst, in0=x, in1=y, op=ALU.mult)
        act = lambda dst, x, func, **kw: nc.scalar.activation(out=dst, in_=x, func=func, **kw)

        def v_mass(t, g):
            nc.vector.scalar_tensor_tensor(
                out=mass_t[t][:, :, 64 * g : 64 * g + 64],
                in0=sig[:, t, :, 64 * g : 64 * g + 64],
                scalar=-1.0,
                in1=xplus[:, t, :, 64 * g : 64 * g + 64],
                op0=ALU.mult,
                op1=ALU.max,
            )

        def v_mc(t, g):
            mult(mc[t][g][:], mass[t][g][:], cx[t, g][:])

        def v_mcc(t, g):
            mult(mcc[t][g][:], mc[t][g][:], cx[t, g][:])
            if g == 0:
                first = bank(2 * t, "sums_a")
                sums[t, 0] = first[:, 0:V]
                for k in range(2):
                    add_up(first[:, P * k : P * k + P], mass[t][k])
            else:
                second = bank(2 * t + 1, "sums_b")
                sums[t, 1], sums[t, 2] = second[:, 0:V], second[:, V : 2 * V]
                for q, src in enumerate((mc, mcc)):
                    for k in range(2):
                        add_up(second[:, V * q + P * k : V * q + P * k + P], src[t][k])

        def s_root(t):
            act(rm[t][:], sums[t, 0], ACT.Abs_reciprocal_sqrt)

        def s_recip(t):
            act(rm[t][:], rm[t][:], ACT.Square)

        def s_mtot(t):
            act(mtot_w[t][:, 0:V], sums[t, 0], ACT.Copy, scale=unit_sb[:, t : t + 1])

        def v_first(t):
            mult(chk[t][:], sums[t, 0], rm[t][:])
            mult(com0[t][:], sums[t, 1], rm[t][:])

        def v_com(t):
            nc.vector.scalar_tensor_tensor(
                out=ncom_w[t][:, 0:V], in0=chk[t][:], scalar=2.0, in1=com0[t][:], op0=ALU.subtract, op1=ALU.mult
            )

        def v_cross(t):
            mult(com0[t][:], sums[t, 1], ncom_w[t][:, 0:V])

        def v_quad(t):
            nc.vector.tensor_tensor(out=quad_w[t][:, 0:V], in0=sums[t, 2], in1=com0[t][:], op=ALU.add)

        def s_com(t):
            act(sep[t][:], ncom_w[t][:].indirect(nd_sb[:]), ACT.Copy)

        def s_quad(t):
            act(g2[t][:], quad_w[t][:].indirect(nd_sb[:]), ACT.Copy)

        def s_mass(t):
            if t == 1:
                late = sbuf([P, 3, U], F32, "mn_late", tag="r4_last")
                mn.update({k: late[:, k - 1, :] for k in range(1, 4)})
            act(mn[t], mtot_w[t][:].indirect(nd_sb[:]), ACT.Copy)

        def v_sep(t):
            nc.vector.tensor_tensor(out=sep[t][:], in0=sep[t][:], in1=px_sb[:, t, :], op=ALU.add)

        def s_sq(t):
            act(r4[t][:], sep[t][:], ACT.Square)

        def s_r4(t):
            act(r4[t][:], r4[t][:], ACT.Square, bias=0.6)

        def s_inv(t):
            act(inv[t][:], r4[t][:], ACT.Abs_reciprocal_sqrt)

        def forces(t):
            mult(sir[t][:], sep[t][:], inv[t][:])
            mult(sep[t][:], sir[t][:], inv[t][:])
            mult(qua[:, t, :], g2[t][:], sep[t][:])

        def v_soft(t):
            nc.vector.scalar_tensor_tensor(
                out=ebuf[:, t, :], in0=qua[:, t, :], scalar=unit_sb[:, t : t + 1], in1=inv[t][:], op0=ALU.mult, op1=ALU.mult
            )

        def v_mono(t):
            mult(mono[:, t, :], mn[t], sir[t][:])

        def do(step, t, *more):
            if 0 <= t < 4:
                step(t, *more)

        v_mass(0, 0)
        for t in range(6):
            do(v_mass, t, 1)
            do(s_root, t - 1)
            do(s_recip, t - 1)
            do(s_mtot, t - 1)
            do(v_mc, t, 0)
            do(forces, t - 4)
            do(v_sep, t - 2)
            do(s_sq, t - 2)
            do(s_r4, t - 2)
            do(s_inv, t - 2)
            do(v_mc, t, 1)
            do(v_first, t - 1)
            do(v_mcc, t, 0)
            do(v_com, t - 1)
            do(s_com, t - 1)
            do(v_mcc, t, 1)
            do(v_cross, t - 1)
            do(v_mass, t + 1, 0)
            do(v_quad, t - 1)
            do(s_quad, t - 1)
        for t in range(2, 4):
            forces(t)
        for t in range(4):
            s_mass(t)
            v_soft(t)
        for t in range(4):
            v_mono(t)
        for c, (r0, n) in enumerate(((0, 128), (128, 128), (256, 128), (384, 128))):
            cols = slice(r0, r0 + n)
            hid = sbuf([P, n, 4], BF16, "hid%d" % c)
            codes = sbuf([P, n], U32, "codes%d" % c)
            hscale = sbuf([P, n], U8, "hscale%d" % c)
            th = sbuf([P, 4, n], F32, "th%d" % c)
            act(th[:], qua[:, :, cols], ACT.Tanh)
            mult(th[:], th[:], mono[:, :, cols])
            nc.vector.tensor_tensor(
                out=hid[:].rearrange("p (c i) t -> p c t i", i=4),
                in0=th[:].rearrange("p t (c i) -> p c t i", i=4),
                in1=ebuf[:, :, cols].rearrange("p t (c i) -> p c t i", i=4),
                op=ALU.subtract,
            )
            nc.vector.quantize_mx(out=codes[:].bitcast(FP8X4), scales=hscale[:], in_=hid[:].rearrange("p r t -> p (r t)"))
            acc = bank(c, "acc")
            for b in range(2):
                nc.tensor.matmul_mx(
                    out=acc[:, n * b : n * b + n],
                    lhsT=w3w[:, 256 * b : 256 * b + 256].bitcast(FP4X4),
                    lhsT_scale=w3s[:, 0, P * b : P * b + P],
                    rhs=codes[:].bitcast(FP8X4),
                    rhs_scale=hscale[:],
                    start=True,
                    stop=True,
                )
            res = sbuf([P, 2, n], F32, "res%d" % c)
            nc.scalar.copy(out=res[:].rearrange("p b r -> p (b r)"), in_=acc[:, 0 : 2 * n])
            nc.sync.dma_start(out=out.rearrange("(b m) r -> m b r", b=2)[:, :, cols], in_=res[:])
